import numpy as np
CORES = [68,69,70,71,76,77,78,79,84,85,86,87,92,93,94,95]
N = 16
def setup_inputs(rng):
    return {"x": rng.standard_normal((N, 128, 4), dtype=np.float32)}
def reference(x):
    s = x.sum(axis=0, dtype=np.float64).astype(x.dtype)
    return {"y": np.broadcast_to(s, (N,) + s.shape)}

@@ -1,0 +1,57 @@
+from concourse.bass import DstId, RemoteDMATransfer
+
+SCRATCH = {
+    "xs": ("dram", [128, 4], "float32"),
+    "gx": ("dram", [4, 128, 4], "float32"),
+    "gp": ("dram", [3, 128, 4], "float32"),
+    "tot": ("dram", [128, 4], "float32"),
+}
+SEMAPHORES = ["loaded", "sent", "got_x", "got_p", "got_tot", "stored"]
+
+HELPER = 2
+MASK_P = (0x03, 0x0C, 0xF0)
+N_P = 2 + 2 + 4
+MASK_T = (0x000F, 0x00F0, 0x0F00, 0xF000)
+
+
+def _dst(topo, c):
+    rid, pid, _se = topo.addr(c)
+    return DstId(rid=rid, pnc=pid)
+
+
+def rank_program(g, core, T, topo):
+    s = T.sem
+    chips = sorted({topo.chip(c) for c in T.cores})
+    ch = topo.chip(core)
+    rank = T.rank_of(core)
+
+    if rank is not None:
+        mine = [c for c in T.cores if topo.chip(c) == ch]
+        rid, pid, _se = topo.addr(ch * 8 + HELPER)
+        g.sync.dma_start(T.xs[:], T.x[:]).then_inc(s.loaded, 16)
+        g.wait_ge(s.loaded, 16)
+        g.remote_dma(T.gx[mine.index(core)], T.xs[:], s.got_x, s.sent, pid, rid, 0xFFFF)
+        g.sync.wait_ge(s.got_tot, 4)
+        g.sync.dma_start(T.y[:], T.tot[:]).then_inc(s.stored, 16)
+        g.sync.wait_ge(s.stored, 16)
+        g.wait_ge(s.sent, 16)
+        return
+
+    if ch not in chips or core % 8 != HELPER:
+        return
+
+    mine = [c for c in T.cores if topo.chip(c) == ch]
+    xs = [T.gx[k] for k in range(4)]
+    peers = (ch ^ 1, ch ^ 2, ch ^ 3)
+    g.wait_ge(s.got_x, 4 * 16)
+    g.remote_dma_fused(
+        [RemoteDMATransfer(dst_ids=[_dst(topo, p * 8 + HELPER)], dma_engine_mask=MASK_P[k], remote_sem=s.got_p,
+                           srcs=xs, dsts=[T.gp[k]], alu_op=1) for k, p in enumerate(peers)],
+        local_sem=s.sent)
+    g.wait_ge(s.got_p, N_P)
+    g.remote_dma_fused(
+        [RemoteDMATransfer(dst_ids=[_dst(topo, c)], dma_engine_mask=MASK_T[k], remote_sem=s.got_tot,
+                           srcs=xs + [T.gp[j] for j in range(3)], dsts=[T.tot[:]], alu_op=1)
+         for k, c in enumerate(mine)],
+        local_sem=s.sent)
+    g.wait_ge(s.sent, N_P + 16)

@@ -2,15 +2,13 @@ from concourse.bass import DstId, RemoteDMATransfer
 
 SCRATCH = {
     "xs": ("dram", [128, 4], "float32"),
-    "gx": ("dram", [4, 128, 4], "float32"),
-    "gp": ("dram", [3, 128, 4], "float32"),
+    "gx": ("dram", [8, 128, 4], "float32"),
+    "gp": ("dram", [128, 4], "float32"),
     "tot": ("dram", [128, 4], "float32"),
 }
 SEMAPHORES = ["loaded", "sent", "got_x", "got_p", "got_tot", "stored"]
 
 HELPER = 2
-MASK_P = (0x03, 0x0C, 0xF0)
-N_P = 2 + 2 + 4
 MASK_T = (0x000F, 0x00F0, 0x0F00, 0xF000)
 
 
@@ -26,11 +24,15 @@ def rank_program(g, core, T, topo):
     rank = T.rank_of(core)
 
     if rank is not None:
-        mine = [c for c in T.cores if topo.chip(c) == ch]
-        rid, pid, _se = topo.addr(ch * 8 + HELPER)
+        slot = 4 * ((ch >> 1) & 1) + [c for c in T.cores if topo.chip(c) == ch].index(core)
         g.sync.dma_start(T.xs[:], T.x[:]).then_inc(s.loaded, 16)
         g.wait_ge(s.loaded, 16)
-        g.remote_dma(T.gx[mine.index(core)], T.xs[:], s.got_x, s.sent, pid, rid, 0xFFFF)
+        g.remote_dma_fused(
+            [RemoteDMATransfer(dst_ids=[_dst(topo, (ch ^ 2) * 8 + HELPER)], dma_engine_mask=0x00FF,
+                               remote_sem=s.got_x, src=T.xs[:], dst=T.gx[slot]),
+             RemoteDMATransfer(dst_ids=[_dst(topo, ch * 8 + HELPER)], dma_engine_mask=0xFF00,
+                               remote_sem=s.got_x, src=T.xs[:], dst=T.gx[slot])],
+            local_sem=s.sent)
         g.sync.wait_ge(s.got_tot, 4)
         g.sync.dma_start(T.y[:], T.tot[:]).then_inc(s.stored, 16)
         g.sync.wait_ge(s.stored, 16)
@@ -40,18 +42,16 @@ def rank_program(g, core, T, topo):
     if ch not in chips or core % 8 != HELPER:
         return
 
+    xs = [T.gx[k] for k in range(8)]
     mine = [c for c in T.cores if topo.chip(c) == ch]
-    xs = [T.gx[k] for k in range(4)]
-    peers = (ch ^ 1, ch ^ 2, ch ^ 3)
-    g.wait_ge(s.got_x, 4 * 16)
+    g.wait_ge(s.got_x, 8 * 8)
     g.remote_dma_fused(
-        [RemoteDMATransfer(dst_ids=[_dst(topo, p * 8 + HELPER)], dma_engine_mask=MASK_P[k], remote_sem=s.got_p,
-                           srcs=xs, dsts=[T.gp[k]], alu_op=1) for k, p in enumerate(peers)],
+        [RemoteDMATransfer(dst_ids=[_dst(topo, (ch ^ 1) * 8 + HELPER)], dma_engine_mask=0x00FF, remote_sem=s.got_p,
+                           srcs=xs, dsts=[T.gp[:]], alu_op=1)],
         local_sem=s.sent)
-    g.wait_ge(s.got_p, N_P)
+    g.wait_ge(s.got_p, 8)
     g.remote_dma_fused(
         [RemoteDMATransfer(dst_ids=[_dst(topo, c)], dma_engine_mask=MASK_T[k], remote_sem=s.got_tot,
-                           srcs=xs + [T.gp[j] for j in range(3)], dsts=[T.tot[:]], alu_op=1)
-         for k, c in enumerate(mine)],
+                           srcs=xs + [T.gp[:]], dsts=[T.tot[:]], alu_op=1) for k, c in enumerate(mine)],
         local_sem=s.sent)
-    g.wait_ge(s.sent, N_P + 16)
+    g.wait_ge(s.sent, 8 + 16)

@@ -9,7 +9,6 @@ SCRATCH = {
 SEMAPHORES = ["loaded", "sent", "got_x", "got_p", "got_tot", "stored"]
 
 HELPER = 2
-MASK_T = (0x000F, 0x00F0, 0x0F00, 0xF000)
 
 
 def _dst(topo, c):
@@ -28,15 +27,14 @@ def rank_program(g, core, T, topo):
         g.sync.dma_start(T.xs[:], T.x[:]).then_inc(s.loaded, 16)
         g.wait_ge(s.loaded, 16)
         g.remote_dma_fused(
-            [RemoteDMATransfer(dst_ids=[_dst(topo, (ch ^ 2) * 8 + HELPER)], dma_engine_mask=0x00FF,
-                               remote_sem=s.got_x, src=T.xs[:], dst=T.gx[slot]),
-             RemoteDMATransfer(dst_ids=[_dst(topo, ch * 8 + HELPER)], dma_engine_mask=0xFF00,
-                               remote_sem=s.got_x, src=T.xs[:], dst=T.gx[slot])],
+            [RemoteDMATransfer(dst_ids=[_dst(topo, (ch ^ 2) * 8 + HELPER), _dst(topo, ch * 8 + HELPER)],
+                               dma_engine_mask=0x00FF, remote_sem=s.got_x,
+                               srcs=[T.xs[:]], dsts=[T.gx[slot], T.gx[slot]])],
             local_sem=s.sent)
-        g.sync.wait_ge(s.got_tot, 4)
+        g.sync.wait_ge(s.got_tot, 16)
         g.sync.dma_start(T.y[:], T.tot[:]).then_inc(s.stored, 16)
         g.sync.wait_ge(s.stored, 16)
-        g.wait_ge(s.sent, 16)
+        g.wait_ge(s.sent, 8)
         return
 
     if ch not in chips or core % 8 != HELPER:
@@ -51,7 +49,7 @@ def rank_program(g, core, T, topo):
         local_sem=s.sent)
     g.wait_ge(s.got_p, 8)
     g.remote_dma_fused(
-        [RemoteDMATransfer(dst_ids=[_dst(topo, c)], dma_engine_mask=MASK_T[k], remote_sem=s.got_tot,
-                           srcs=xs + [T.gp[:]], dsts=[T.tot[:]], alu_op=1) for k, c in enumerate(mine)],
+        [RemoteDMATransfer(dst_ids=[_dst(topo, c) for c in mine], dma_engine_mask=0xFFFF, remote_sem=s.got_tot,
+                           srcs=xs + [T.gp[:]], dsts=[T.tot[:] for c in mine], alu_op=1)],
         local_sem=s.sent)
     g.wait_ge(s.sent, 8 + 16)

@@ -8,8 +8,6 @@ SCRATCH = {
 }
 SEMAPHORES = ["loaded", "sent", "got_x", "got_p", "got_tot", "stored"]
 
-HELPER = 2
-
 
 def _dst(topo, c):
     rid, pid, _se = topo.addr(c)
@@ -18,38 +16,34 @@ def _dst(topo, c):
 
 def rank_program(g, core, T, topo):
     s = T.sem
-    chips = sorted({topo.chip(c) for c in T.cores})
     ch = topo.chip(core)
-    rank = T.rank_of(core)
-
-    if rank is not None:
-        slot = 4 * ((ch >> 1) & 1) + [c for c in T.cores if topo.chip(c) == ch].index(core)
-        g.sync.dma_start(T.xs[:], T.x[:]).then_inc(s.loaded, 16)
-        g.wait_ge(s.loaded, 16)
-        g.remote_dma_fused(
-            [RemoteDMATransfer(dst_ids=[_dst(topo, (ch ^ 2) * 8 + HELPER), _dst(topo, ch * 8 + HELPER)],
-                               dma_engine_mask=0x00FF, remote_sem=s.got_x,
-                               srcs=[T.xs[:]], dsts=[T.gx[slot], T.gx[slot]])],
-            local_sem=s.sent)
-        g.sync.wait_ge(s.got_tot, 16)
-        g.sync.dma_start(T.y[:], T.tot[:]).then_inc(s.stored, 16)
-        g.sync.wait_ge(s.stored, 16)
+    if T.rank_of(core) is None:
+        return
+    k = core % 8
+    slot = 4 * ((ch >> 1) & 1) + (k - 4)
+    to = [c for c in ((ch ^ 2) * 8 + 6, (ch ^ 2) * 8 + 7, ch * 8 + 6, ch * 8 + 7) if c != core]
+    g.sync.dma_start(T.xs[:], T.x[:]).then_inc(s.loaded, 16)
+    g.wait_ge(s.loaded, 16)
+    g.remote_dma_fused(
+        [RemoteDMATransfer(dst_ids=[_dst(topo, c) for c in to], dma_engine_mask=0x00FF, remote_sem=s.got_x,
+                           srcs=[T.xs[:]], dsts=[T.gx[slot] for c in to])],
+        local_sem=s.sent)
+    g.sync.wait_ge(s.got_tot, 16)
+    g.sync.dma_start(T.y[:], T.tot[:]).then_inc(s.stored, 16)
+    g.sync.wait_ge(s.stored, 16)
+    if k < 6:
         g.wait_ge(s.sent, 8)
         return
-
-    if ch not in chips or core % 8 != HELPER:
-        return
-
-    xs = [T.gx[k] for k in range(8)]
-    mine = [c for c in T.cores if topo.chip(c) == ch]
-    g.wait_ge(s.got_x, 8 * 8)
+    xs = [T.xs[:] if j == slot else T.gx[j] for j in range(8)]
+    serve = (ch * 8 + 4, ch * 8 + 7) if k == 6 else (ch * 8 + 5, ch * 8 + 6)
+    g.wait_ge(s.got_x, 7 * 8)
     g.remote_dma_fused(
-        [RemoteDMATransfer(dst_ids=[_dst(topo, (ch ^ 1) * 8 + HELPER)], dma_engine_mask=0x00FF, remote_sem=s.got_p,
+        [RemoteDMATransfer(dst_ids=[_dst(topo, (ch ^ 1) * 8 + k)], dma_engine_mask=0x00FF, remote_sem=s.got_p,
                            srcs=xs, dsts=[T.gp[:]], alu_op=1)],
         local_sem=s.sent)
     g.wait_ge(s.got_p, 8)
     g.remote_dma_fused(
-        [RemoteDMATransfer(dst_ids=[_dst(topo, c) for c in mine], dma_engine_mask=0xFFFF, remote_sem=s.got_tot,
-                           srcs=xs + [T.gp[:]], dsts=[T.tot[:] for c in mine], alu_op=1)],
+        [RemoteDMATransfer(dst_ids=[_dst(topo, c) for c in serve], dma_engine_mask=0xFFFF, remote_sem=s.got_tot,
+                           srcs=xs + [T.gp[:]], dsts=[T.tot[:] for c in serve], alu_op=1)],
         local_sem=s.sent)
-    g.wait_ge(s.sent, 8 + 16)
+    g.wait_ge(s.sent, 8 + 8 + 16)

@@ -3,7 +3,7 @@ from concourse.bass import DstId, RemoteDMATransfer
 SCRATCH = {
     "xs": ("dram", [128, 4], "float32"),
     "gx": ("dram", [8, 128, 4], "float32"),
-    "gp": ("dram", [128, 4], "float32"),
+    "gp": ("dram", [2, 128, 4], "float32"),
     "tot": ("dram", [128, 4], "float32"),
 }
 SEMAPHORES = ["loaded", "sent", "got_x", "got_p", "got_tot", "stored"]
@@ -14,36 +14,45 @@ def _dst(topo, c):
     return DstId(rid=rid, pnc=pid)
 
 
+def _send(g, topo, sem_r, sem_l, srcs, to, out, mask):
+    g.remote_dma_fused(
+        [RemoteDMATransfer(dst_ids=[_dst(topo, c) for c in to], dma_engine_mask=mask, remote_sem=sem_r,
+                           srcs=srcs, dsts=[out for c in to], alu_op=1 if len(srcs) > 1 else 0)],
+        local_sem=sem_l)
+
+
 def rank_program(g, core, T, topo):
     s = T.sem
     ch = topo.chip(core)
     if T.rank_of(core) is None:
         return
     k = core % 8
-    slot = 4 * ((ch >> 1) & 1) + (k - 4)
-    to = [c for c in ((ch ^ 2) * 8 + 6, (ch ^ 2) * 8 + 7, ch * 8 + 6, ch * 8 + 7) if c != core]
+    base = 4 * ((ch >> 1) & 1)
+    slot = base + (k - 4)
+    plane, mate = (ch ^ 2) * 8, (ch ^ 1) * 8
+
     g.sync.dma_start(T.xs[:], T.x[:]).then_inc(s.loaded, 16)
     g.wait_ge(s.loaded, 16)
-    g.remote_dma_fused(
-        [RemoteDMATransfer(dst_ids=[_dst(topo, c) for c in to], dma_engine_mask=0x00FF, remote_sem=s.got_x,
-                           srcs=[T.xs[:]], dsts=[T.gx[slot] for c in to])],
-        local_sem=s.sent)
+    to = [c for c in (plane + 6, ch * 8 + 6, ch * 8 + 7) if c != core]
+    _send(g, topo, s.got_x, s.sent, [T.xs[:]], to, T.gx[slot], 0x00FF)
+
     g.sync.wait_ge(s.got_tot, 16)
     g.sync.dma_start(T.y[:], T.tot[:]).then_inc(s.stored, 16)
     g.sync.wait_ge(s.stored, 16)
-    if k < 6:
+
+    if k == 6:
+        raw = [T.xs[:] if j == slot else T.gx[j] for j in range(8)]
+        g.wait_ge(s.got_x, 7 * 8)
+        _send(g, topo, s.got_p, s.sent, raw, [mate + 6, mate + 7], T.gp[0], 0x00FF)
+        g.wait_ge(s.got_p, 8)
+        _send(g, topo, s.got_tot, s.sent, raw + [T.gp[0]], [ch * 8 + 4, ch * 8 + 7], T.tot[:], 0xFFFF)
+        g.wait_ge(s.sent, 8 + 8 + 16)
+    elif k == 7:
+        raw = [T.xs[:] if j == slot else T.gx[j] for j in range(base, base + 4)]
+        g.wait_ge(s.got_x, 3 * 8)
+        _send(g, topo, s.got_p, s.sent, raw, [plane + 7], T.gp[1], 0x00FF)
+        g.wait_ge(s.got_p, 8 + 8)
+        _send(g, topo, s.got_tot, s.sent, raw + [T.gp[0], T.gp[1]], [ch * 8 + 5, ch * 8 + 6], T.tot[:], 0xFFFF)
+        g.wait_ge(s.sent, 8 + 8 + 16)
+    else:
         g.wait_ge(s.sent, 8)
-        return
-    xs = [T.xs[:] if j == slot else T.gx[j] for j in range(8)]
-    serve = (ch * 8 + 4, ch * 8 + 7) if k == 6 else (ch * 8 + 5, ch * 8 + 6)
-    g.wait_ge(s.got_x, 7 * 8)
-    g.remote_dma_fused(
-        [RemoteDMATransfer(dst_ids=[_dst(topo, (ch ^ 1) * 8 + k)], dma_engine_mask=0x00FF, remote_sem=s.got_p,
-                           srcs=xs, dsts=[T.gp[:]], alu_op=1)],
-        local_sem=s.sent)
-    g.wait_ge(s.got_p, 8)
-    g.remote_dma_fused(
-        [RemoteDMATransfer(dst_ids=[_dst(topo, c) for c in serve], dma_engine_mask=0xFFFF, remote_sem=s.got_tot,
-                           srcs=xs + [T.gp[:]], dsts=[T.tot[:] for c in serve], alu_op=1)],
-        local_sem=s.sent)
-    g.wait_ge(s.sent, 8 + 8 + 16)

from concourse.bass import DstId, RemoteDMATransfer

SCRATCH = {
    "xs": ("dram", [128, 4], "float32"),
    "gx": ("dram", [8, 128, 4], "float32"),
    "gp": ("dram", [2, 128, 4], "float32"),
    "tot": ("dram", [128, 4], "float32"),
}
SEMAPHORES = ["loaded", "sent", "got_x", "got_p", "got_tot", "stored"]


def _dst(topo, c):
    rid, pid, _se = topo.addr(c)
    return DstId(rid=rid, pnc=pid)


def _send(g, topo, sem_r, sem_l, srcs, to, out, mask):
    g.remote_dma_fused(
        [RemoteDMATransfer(dst_ids=[_dst(topo, c) for c in to], dma_engine_mask=mask, remote_sem=sem_r,
                           srcs=srcs, dsts=[out for c in to], alu_op=1 if len(srcs) > 1 else 0)],
        local_sem=sem_l)


def rank_program(g, core, T, topo):
    s = T.sem
    ch = topo.chip(core)
    if T.rank_of(core) is None:
        return
    k = core % 8
    base = 4 * ((ch >> 1) & 1)
    slot = base + (k - 4)
    plane, mate = (ch ^ 2) * 8, (ch ^ 1) * 8

    g.sync.dma_start(T.xs[:], T.x[:]).then_inc(s.loaded, 16)
    g.wait_ge(s.loaded, 16)
    to = [c for c in (plane + 6, ch * 8 + 6, ch * 8 + 7) if c != core]
    _send(g, topo, s.got_x, s.sent, [T.xs[:]], to, T.gx[slot], 0x00FF)

    g.sync.wait_ge(s.got_tot, 16)
    g.sync.dma_start(T.y[:], T.tot[:]).then_inc(s.stored, 16)
    g.sync.wait_ge(s.stored, 16)

    if k == 6:
        raw = [T.xs[:] if j == slot else T.gx[j] for j in range(8)]
        g.wait_ge(s.got_x, 7 * 8)
        _send(g, topo, s.got_p, s.sent, raw, [mate + 6, mate + 7], T.gp[0], 0x00FF)
        g.wait_ge(s.got_p, 8)
        _send(g, topo, s.got_tot, s.sent, raw + [T.gp[0]], [ch * 8 + 4, ch * 8 + 7], T.tot[:], 0xFFFF)
        g.wait_ge(s.sent, 8 + 8 + 16)
    elif k == 7:
        raw = [T.xs[:] if j == slot else T.gx[j] for j in range(base, base + 4)]
        g.wait_ge(s.got_x, 3 * 8)
        _send(g, topo, s.got_p, s.sent, raw, [plane + 7], T.gp[1], 0x00FF)
        g.wait_ge(s.got_p, 8 + 8)
        _send(g, topo, s.got_tot, s.sent, raw + [T.gp[0], T.gp[1]], [ch * 8 + 5, ch * 8 + 6], T.tot[:], 0xFFFF)
        g.wait_ge(s.sent, 8 + 8 + 16)
    else:
        g.wait_ge(s.sent, 8)
